import numpy as np
import ml_dtypes


def mxq(x, axis, fmt="e4m3"):
    dtype, down = {"e4m3": (ml_dtypes.float8_e4m3fn, 7), "e5m2": (ml_dtypes.float8_e5m2, 14)}[fmt]
    v = np.moveaxis(np.asarray(x, np.float32).astype(ml_dtypes.bfloat16).astype(np.float64), axis, -1)
    blocks = v.reshape(v.shape[:-1] + (-1, 32))
    amax = np.abs(blocks).max(-1, keepdims=True)
    byte = np.maximum(np.where(amax > 0, np.frexp(amax)[1] - 1 + 127, 0) - down, 1)
    scale = np.exp2(byte - 127.0)
    codes = (blocks / scale).astype(np.float32).astype(dtype).astype(np.float64)
    return np.moveaxis((codes * scale).reshape(v.shape), -1, axis)


WIDE = False


def mx_kscale(k):
    if not WIDE:
        return np.ones(k)
    levels = np.array([18, -18])
    if k % 512:
        return np.exp2(np.random.permutation(np.resize(levels, k // 32))).repeat(32)
    a = np.empty((k // 512, 16))
    for p in range(k // 512):
        a[p, :8] = np.random.permutation(np.resize(levels, 8))
        for g in range(8):
            far = levels[np.abs(levels - a[p, g]) >= 10]
            a[p, g + 8] = far[np.random.randint(len(far))]
    return np.exp2(a.ravel()).repeat(32)


def f64(x):
    return np.asarray(x).astype(np.float64)


def striped(idx):
    return np.tile(np.asarray(idx).reshape(-1, 16).T, (8, 1)).astype(np.uint16)


def unstriped(offs):
    return offs[:16].T.reshape(-1).astype(np.int64)

def planes(y):
    n, m = y.shape
    v = y.astype(np.float32).astype(ml_dtypes.bfloat16).astype(np.float64).reshape(n // 32, 32, m)
    top = np.abs(v).max(1)
    byte = np.clip(np.where(top > 0, np.frexp(top)[1] - 1 + 127 - 7, 1), 1, 254)
    codes = (v * np.exp2(127.0 - byte)[:, None, :]).reshape(n, m).astype(np.float32).astype(ml_dtypes.float8_e4m3fn).view(np.uint8)
    words = codes.reshape(n // 512, 128, 4, m).transpose(0, 1, 3, 2)
    return np.ascontiguousarray(words), np.ascontiguousarray(byte.astype(np.uint8).reshape(n // 512, 16, m))


def setup_inputs():
    n = np.random.standard_normal
    uni = np.random.uniform
    idx = np.random.permutation(2048)[:512]
    f_d = mx_kscale(512)
    f_r = mx_kscale(512)
    return {
        "vT": (n((512, 2048)) * f_d[:, None]).astype(np.float32),
        "x": (n((512, 512)) / np.sqrt(512) * f_r[:, None] / f_d[None, :]).astype(np.float32),
        "cs": np.tile(uni(0.75, 1.3, 512) / f_d, (128, 1)).astype(np.float32),
        "gl": np.tile(uni(10.0, 30.0, 2048), (128, 1)).astype(np.float32),
        "y": (n((512, 512))).astype(np.float32),
        "us": (uni(0.75, 1.3, (512, 1)) / f_r[:, None]).astype(np.float32),
        "wt": (uni(0.75, 1.3, (512, 1)) / np.sqrt(512)).astype(np.float32),
        "offs": striped(idx),
    }


def reference(vT, x, cs, gl, y, us, wt, offs):
    idx = unstriped(offs)
    vT_i = f64(vT)[:, idx]
    gl_i = f64(gl)[:1][:, idx]
    gc = gl_i.T
    vt = vT_i.T
    nn = (np.square(f64(cs)[:1] * vt)).sum(-1, keepdims=True)
    len = np.sqrt(nn)
    lr = len.T
    a = mxq(f64(x), 1, "e4m3") @ mxq(vT_i, 0, "e4m3")
    g = f64(wt) * f64(us) * (f64(us) * gl_i * a / lr - f64(y))
    b = mxq(g, 0, "e5m2").T @ mxq(f64(x), 0, "e4m3")
    dg = (b * vt).sum(-1, keepdims=True)
    dvt = gc / len * (b - dg / nn * np.square(f64(cs)[:1]) * vt)
    dvd = dvt.T
    out_0 = np.zeros((512, 2048))
    out_0[:, idx] = dvd
    return (out_0,) + planes(out_0)

@@ -1,0 +1,350 @@
+import concourse.mybir as mybir
+from concourse.masks import make_identity
+
+FLOPS = 536870912
+
+F32 = mybir.dt.float32
+BF16 = mybir.dt.bfloat16
+I32 = mybir.dt.int32
+U32 = mybir.dt.uint32
+U16 = mybir.dt.uint16
+U8 = mybir.dt.uint8
+E4M3 = mybir.dt.float8_e4m3fn_x4
+E5M2 = mybir.dt.float8_e5m2_x4
+MULT = mybir.AluOpType.mult
+ADD = mybir.AluOpType.add
+SUBTRACT = mybir.AluOpType.subtract
+COPY = mybir.ActivationFunctionType.Copy
+SQUARE = mybir.ActivationFunctionType.Square
+SQRT = mybir.ActivationFunctionType.Sqrt
+
+P = 128
+L = 4
+N = 512
+T = 2048
+H = 256
+C = 512
+NV = 2
+YC = "vs"
+
+
+def tile_attend_gwnorm_v_pl_kernel(tc, vT, x, cs, gl, y, us, wt, offs, out_0, out_1, out_2):
+    nc = tc.nc
+    with tc.tile_pool(name="keep", bufs=1) as keep, tc.psum_pool(name="psum", bufs=1) as psum:
+
+        def sb(name, shape, dtype=F32, tag=None):
+            return keep.tile(shape, dtype, name=name, tag=tag or name, align_bytes=64)
+
+        def bank(n, name, shape):
+            return psum.tile(shape, F32, name=name, tag="bank%d" % n)
+
+        def blk(m):
+            return slice(m * P, (m + 1) * P)
+
+        offsets = keep.tile([P, N // 16], U16, name="offsets")
+        nc.sync.dma_start(offsets[:], offs)
+
+        v_rows = vT.rearrange("(p t) c -> p t c", t=L)
+        v_plane = [sb("v_plane%d" % t, [P, T]) for t in range(L)]
+        cs_col = sb("cs_col", [P, L])
+        us_col = sb("us_col", [P, L])
+        wt_col = sb("wt_col", [P, L])
+        gl_one = sb("gl_one", [1, T], tag="dv")
+        nc.sync.dma_start(gl_one[:], gl[0:1, :])
+        nc.sync.dma_start(v_plane[0][:], v_rows[:, 0, :])
+        nc.sync.dma_start(cs_col[:], cs[0:1, :].rearrange("o (p t) -> p (o t)", t=L))
+        nc.sync.dma_start(us_col[:], us.rearrange("(p j) o -> p (j o)", j=L))
+        nc.sync.dma_start(wt_col[:], wt.rearrange("(p j) o -> p (j o)", j=L))
+        for t in range(1, L):
+            nc.sync.dma_start(v_plane[t][:], v_rows[:, t, :])
+        x_rows = x.rearrange("(p j) d -> p j d", j=L)
+        x_sb = sb("x_sb", [P, L, N])
+        for j in range(L):
+            nc.sync.dma_start(x_sb[:, j, :], x_rows[:, j, :])
+
+        root_warm = sb("root_warm", [P, 8])
+        nc.gpsimd.memset(root_warm[:, 0:1], 1.0)
+        nc.scalar.activation(root_warm[:, 4:5], root_warm[:, 0:1], SQRT)
+
+        gl_win = sb("gl_win", [P, T])
+        nc.gpsimd.memset(gl_win[:], 0.0)
+        nc.scalar.activation(gl_win[0:1, :], gl_one[:], COPY)
+
+        y_rows = y.rearrange("(p j) i -> p j i", j=L)
+        y_sb = [sb("y_sb%d" % h, [P, L, H]) for h in range(2)]
+        for h in range(2):
+            nc.sync.dma_start(y_sb[h][:], y_rows[:, :, h * H:(h + 1) * H])
+
+        ident = sb("ident", [P, P])
+        make_identity(nc, ident[:])
+
+        win = [sb("win%d" % t, [P, T]) for t in range(L)]
+        for t in range(L):
+            nc.gpsimd.memset(win[t][:], 0.0)
+
+        cs2_col = sb("cs2_col", [P, L])
+        c2_col = sb("c2_col", [P, L])
+        c1_col = sb("c1_col", [P, L])
+        nc.vector.tensor_tensor(cs2_col[:], cs_col[:], cs_col[:], MULT)
+        nc.vector.tensor_tensor(c2_col[:], wt_col[:], us_col[:], MULT)
+        nc.vector.tensor_tensor(c1_col[:], c2_col[:], us_col[:], MULT)
+
+        g_all = [sb("g_all%d" % u, [P, 2 * N]) for u in range(2)]
+        vb = [sb("vb%d" % h, [P, H, L], BF16) for h in range(2)]
+        cs2_ps = bank(4, "cs2_ps", [P, L, P])
+        for t in range(L):
+            nc.tensor.transpose(cs2_ps[:, t, :], cs2_col[:, t:t + 1].to_broadcast([P, P]), ident[:])
+        cs2_row = sb("cs2_row", [P, N])
+        nc.scalar.copy(cs2_row[:], cs2_ps[:].rearrange("p t q -> p (t q)"))
+        nn_ps = [bank(m, "nn_ps%d" % m, [P, P]) for m in range(L)]
+        sq = [sb("sq%d" % t, [P, N]) for t in range(L)]
+
+        def gathered(t, lo, hi):
+            return g_all[t // 2][:, (t % 2) * N + lo * P:(t % 2) * N + hi * P]
+
+        def gather_v(t, lo, hi):
+            nc.vector.tensor_copy(gathered(t, lo, hi), v_plane[t][:].indirect(offsets[:, lo * 8:hi * 8]))
+
+        def squares(t, lo, hi):
+            nc.scalar.activation(sq[t][:, lo * P:hi * P], gathered(t, lo, hi), SQUARE, scale=cs_col[:, t:t + 1])
+            for m in range(lo, hi):
+                nc.tensor.matmul(nn_ps[m][:], sq[t][:, blk(m)], ident[:], start=(t == 0), stop=(t == L - 1), is_transpose=True)
+
+        def round_pair(u, h):
+            dst = vb[h][:, :, 2 * u:2 * u + 2].rearrange("p (c i) e -> p c e i", i=4)
+            src = g_all[u][:].rearrange("p (e n) -> p e n", e=2)[:, :, h * H:(h + 1) * H].rearrange("p e (c i) -> p c e i", i=4)
+            if u == 0:
+                nc.scalar.copy(dst, src)
+            else:
+                nc.vector.tensor_copy(dst, src)
+
+        for t in range(3):
+            gather_v(t, 0, L)
+            if t == 0:
+                gl_row = sb("gl_row", [P, N])
+                nc.vector.tensor_copy(gl_row[:], gl_win[:].indirect(offsets[:]))
+                gl_ps = bank(6, "gl_ps", [P, L, P])
+                for m in range(L):
+                    nc.tensor.transpose(gl_ps[:, m, :], gl_row[:, blk(m)], ident[:])
+                gl_col = sb("gl_col", [P, L])
+                nc.vector.tensor_copy(gl_col[:], gl_ps[:, :, 0])
+            squares(t, 0, L)
+            if t == 1:
+                round_pair(0, 0)
+                round_pair(0, 1)
+
+        vq = [sb("vq%d" % h, [P, H], U32) for h in range(2)]
+        vs = [sb("vs%d" % h, [P, H], U8) for h in range(2)]
+        nn = [sb("nn%d" % h, [P, 2]) for h in range(2)]
+        nn_junk = sb("nn_junk", [P, N])
+        length = [sb("length%d" % h, [P, 2]) for h in range(2)]
+        rlen = [sb("rlen%d" % h, [P, 2]) for h in range(2)]
+        s_col = [sb("s_col%d" % h, [P, 2]) for h in range(2)]
+        nrnn = [sb("nrnn%d" % h, [P, 2]) for h in range(2)]
+        s_row = [sb("s_row%d" % h, [P, H]) for h in range(2)]
+        yc = [sb("yc%d" % h, [P, L, H]) for h in range(2)]
+        a_ps = [None] * L
+
+        def lengths(h):
+            for e in range(2):
+                nc.scalar.activation(nn_junk[:, blk(2 * h + e)], nn_ps[2 * h + e][:], COPY, accum_out=nn[h][:, e:e + 1])
+            nc.scalar.activation(length[h][:], nn[h][:], SQRT)
+            nc.vector.reciprocal(rlen[h][:], length[h][:])
+            nc.vector.tensor_tensor(s_col[h][:], rlen[h][:], gl_col[:, 2 * h:2 * h + 2], MULT)
+            s_ps = bank(4 + h, "s_ps%d" % h, [P, 2, P])
+            for e in range(2):
+                nc.tensor.transpose(s_ps[:, e, :], s_col[h][:, e:e + 1].to_broadcast([P, P]), ident[:])
+            nc.scalar.copy(s_row[h][:], s_ps[:].rearrange("p m i -> p (m i)"))
+
+        def first(h):
+            round_pair(1, h)
+            nc.vector.quantize_mx(vq[h][:].bitcast(E4M3), vs[h][:], vb[h][:].rearrange("p i t -> p (i t)"))
+
+        def first_mm(h):
+            for u in range(2):
+                a_ps[2 * h + u] = bank(2 * h + u, "a_ps%d_%d" % (h, u), [P, 2, H])
+                for e in range(2):
+                    j = 2 * u + e
+                    nc.tensor.matmul_mx(a_ps[2 * h + u][:, e, :], lhsT=xq[j][:].bitcast(E4M3), lhsT_scale=xs[j][:], rhs=vq[h][:].bitcast(E4M3), rhs_scale=vs[h][:], start=True, stop=True)
+
+        xq = [sb("xq%d" % j, [P, P], U32) for j in range(L)]
+        xs = [sb("xs%d" % j, [P, P], U8) for j in range(L)]
+
+        def x_along_d(j):
+            xb = sb("xb%d" % j, [P, 2, P, 2], BF16)
+            nc.vector.tensor_copy(xb[:].rearrange("p u q e -> p q u e"), x_sb[:, j, :].rearrange("p (q u e) -> p q u e", u=2, e=2))
+            words = xb[:].rearrange("p u q e -> p (u q e)").bitcast(F32)
+            ps = bank(6 + j % 2, "xt_ps%d" % j, [P, 2, P])
+            for u in range(2):
+                nc.tensor.transpose(ps[:, u, :], words[:, blk(u)], ident[:])
+            xtb = sb("xtb%d" % j, [P, N], BF16)
+            nc.scalar.copy(xtb[:].bitcast(F32).rearrange("q (p u) -> q p u", u=2), ps[:].rearrange("q u p -> q p u"))
+            nc.vector.quantize_mx(xq[j][:].bitcast(E4M3), xs[j][:], xtb[:])
+
+        for h in range(2):
+            gather_v(3, 2 * h, 2 * h + 2)
+            squares(3, 2 * h, 2 * h + 2)
+        lengths(0)
+        first(0)
+        for j in range(L):
+            x_along_d(j)
+        first_mm(0)
+        lengths(1)
+        first(1)
+        first_mm(1)
+
+        def scale_y(h):
+            for j in range(L):
+                if YC[h] == "g":
+                    nc.gpsimd.tensor_scalar(yc[h][:, j, :], y_sb[h][:, j, :], c2_col[:, j:j + 1], 0.0, MULT, ADD)
+                elif YC[h] == "s":
+                    nc.scalar.activation(yc[h][:, j, :], y_sb[h][:, j, :], COPY, scale=c2_col[:, j:j + 1])
+                else:
+                    nc.vector.tensor_scalar(yc[h][:, j, :], y_sb[h][:, j, :], c2_col[:, j:j + 1], None, MULT)
+
+        scale_y(0)
+        xrb = sb("xrb", [P, L, P, L], BF16)
+        for k in range(8):
+            qs = slice(16 * k, 16 * (k + 1))
+            nc.scalar.copy(xrb[:, :, qs, :].rearrange("p t q j -> p q j t"), x_sb[:].rearrange("p j (q t) -> p q j t", t=L)[:, qs, :, :])
+        xrq = sb("xrq", [P, N], U32)
+        xrs = sb("xrs", [P, N], U8)
+
+        scale_y(1)
+        for h in range(2):
+            nc.vector.scalar_tensor_tensor(nrnn[h][:], rlen[h][:], -1.0, rlen[h][:], MULT, MULT)
+
+        vt_ps = [None] * L
+
+        def turn_v(h):
+            for e in range(2):
+                m = 2 * h + e
+                vt_ps[m] = bank([4, 5, 0, 1][m], "vt_ps%d" % m, [P, L, P])
+                for t in range(L):
+                    nc.tensor.transpose(vt_ps[m][:, t, :], gathered(t, m, m + 1), ident[:])
+
+        gq = [sb("gq%d" % h, [P, H], U32) for h in range(2)]
+        gs = [sb("gs%d" % h, [P, H], U8) for h in range(2)]
+        gb = [sb("gb%d" % h, [P, H, L], BF16) for h in range(2)]
+        t1 = [sb("t1_%d" % h, [P, L, H]) for h in range(2)]
+        sbv = [sb("sb%d" % m, [P, N]) for m in range(L)]
+        uv = [sb("u%d" % m, [P, N]) for m in range(L)]
+        junk = [sb("junk%d" % m, [P, N], tag="sq%d" % m) for m in range(L)]
+        k_col = [sb("k%d" % m, [P, 1]) for m in range(L)]
+        dv_all = sb("dv", [P, L * N])
+        dv = [dv_all[:, t * N:(t + 1) * N] for t in range(L)]
+
+        def scale_a(h):
+            for j in range(L):
+                nc.vector.scalar_tensor_tensor(t1[h][:, j, :], a_ps[2 * h + j // 2][:, j % 2, :], c1_col[:, j:j + 1], s_row[h][:], MULT, MULT)
+
+        def make_g(h):
+            nc.vector.tensor_tensor(gb[h][:].rearrange("p (c i) j -> p c j i", i=4), t1[h][:].rearrange("p j (c i) -> p c j i", i=4), yc[h][:].rearrange("p j (c i) -> p c j i", i=4), SUBTRACT)
+
+        def second_q(h):
+            nc.vector.quantize_mx(gq[h][:].bitcast(E5M2), gs[h][:], gb[h][:].rearrange("p i j -> p (i j)"))
+
+        def second(h):
+            for e in range(2):
+                m = 2 * h + e
+                b_ps = bank(6 + e, "b_ps%d" % m, [P, N])
+                nc.tensor.matmul_mx(b_ps[:], lhsT=gq[h][:, blk(e)].bitcast(E5M2), lhsT_scale=gs[h][:, blk(e)], rhs=xrq[:].bitcast(E4M3), rhs_scale=xrs[:], start=True, stop=True)
+                nc.scalar.activation(sbv[m][:], b_ps[:], COPY, scale=s_col[h][:, e:e + 1])
+
+        def project(h):
+            for e in range(2):
+                m = 2 * h + e
+                nc.vector.scalar_tensor_tensor(junk[m][:], vt_ps[m][:].rearrange("p t q -> p (t q)"), nrnn[h][:, e:e + 1], sbv[m][:], MULT, MULT, accum_out=k_col[m][:])
+            for e in range(2):
+                m = 2 * h + e
+                nc.vector.scalar_tensor_tensor(uv[m][:], vt_ps[m][:].rearrange("p t q -> p (t q)"), k_col[m][:], cs2_row[:], MULT, MULT)
+
+        def turn_back(ps, t, ms):
+            for n, m in enumerate(ms):
+                nc.tensor.matmul(ps[:, n, :], sbv[m][:, blk(t)], ident[:], start=True, stop=False, is_transpose=True)
+                nc.tensor.matmul(ps[:, n, :], uv[m][:, blk(t)], ident[:], start=False, stop=True, is_transpose=True)
+
+        def out_part(t, lo, hi, n):
+            ps = bank(n, "o_ps%d_%d" % (t, lo), [P, hi - lo, P])
+            turn_back(ps, t, range(lo, hi))
+            nc.scalar.copy(dv[t][:, lo * P:hi * P], ps[:].rearrange("p m i -> p (m i)"))
+
+        def scatter(t, lo, hi):
+            nc.vector.tensor_copy(win[t][:].indirect(offsets[:, lo * 8:hi * 8]), dv[t][:, lo * P:hi * P])
+
+        o_rows = out_0.rearrange("(p t) c -> p t c", t=L)
+        edges = [0, 256, 512, 1024, 1536, 2048]
+        chunks = [(edges[c], edges[c + 1]) for c in range(5)]
+        pairs = [sb("pairs%d" % c, [P, 2, hi - lo, 2], BF16, tag=["v_plane0", "v_plane1", "v_plane2", "v_plane3", "gl_win"][c]) for c, (lo, hi) in enumerate(chunks)]
+
+        def round_plane(t):
+            for c, (lo, hi) in enumerate(chunks):
+                if t >= 2 and c < NV:
+                    nc.vector.tensor_copy(pairs[c][:, t // 2, :, t % 2], win[t][:, lo:hi])
+                else:
+                    nc.scalar.copy(pairs[c][:, t // 2, :, t % 2], win[t][:, lo:hi])
+
+        scale_a(0)
+        make_g(0)
+        nc.vector.quantize_mx(xrq[:].bitcast(E4M3), xrs[:], xrb[:].rearrange("p t q j -> p (t q j)"))
+        second_q(0)
+        second(0)
+        turn_v(0)
+        scale_a(1)
+        make_g(1)
+        second_q(1)
+        turn_v(1)
+        project(0)
+        second(1)
+        out_part(0, 0, 2, 2)
+        project(1)
+        scatter(0, 0, 2)
+        out_part(0, 2, 4, 3)
+        out_part(1, 0, 4, 4)
+        out_part(2, 0, 4, 5)
+        out_part(3, 0, 4, 6)
+        scatter(0, 2, 4)
+        nc.sync.dma_start(o_rows[:, 0, :], win[0][:])
+        round_plane(0)
+        scatter(1, 0, 4)
+        nc.sync.dma_start(o_rows[:, 1, :], win[1][:])
+        round_plane(1)
+        scatter(2, 0, 4)
+        nc.sync.dma_start(o_rows[:, 2, :], win[2][:])
+        round_plane(2)
+        scatter(3, 0, 4)
+        nc.sync.dma_start(o_rows[:, 3, :], win[3][:])
+
+        o_words = out_1[0].rearrange("p c l -> p (c l)").bitcast(I32)
+        o_scales = sb("o_scales", [P, T], U8)
+        ob = [sb("ob%d" % c, [P, (hi - lo) * L], BF16) for c, (lo, hi) in enumerate(chunks)]
+        oq = [sb("oq%d" % k, [P, C], U32) for k in range(4)]
+
+        def weave(c, eng):
+            dst = ob[c][:].bitcast(F32).rearrange("p (c i u) -> p c u i", i=4, u=2)
+            src = pairs[c][:].rearrange("p u c e -> p (u c e)").bitcast(F32).rearrange("p (u c i) -> p c u i", u=2, i=4)
+            if eng == "v":
+                nc.vector.tensor_copy(dst, src)
+            else:
+                nc.scalar.copy(dst, src)
+
+        def finish(c):
+            lo, hi = chunks[c]
+            k = lo // C
+            nc.vector.quantize_mx(oq[k][:, lo - k * C:hi - k * C].bitcast(E4M3), o_scales[:, lo:hi], ob[c][:])
+            if hi % C == 0:
+                nc.sync.dma_start(o_words[:, k * C:(k + 1) * C], oq[k][:].bitcast(I32))
+
+        round_plane(3)
+        weave(0, "v")
+        weave(1, "v")
+        finish(0)
+        weave(2, "v")
+        finish(1)
+        weave(4, "s")
+        weave(3, "v")
+        finish(2)
+        finish(3)
+        finish(4)
+        for q in range(4):
+            (nc.scalar if q % 2 else nc.sync).dma_start(out_2[0, 4 * q:4 * q + 4, :].bitcast(I32), o_scales[32 * q:32 * q + 4, :].bitcast(I32))

@@ -53,21 +53,21 @@ def tile_attend_gwnorm_v_pl_kernel(tc, vT, x, cs, gl, y, us, wt, offs, out_0, ou
         nc.sync.dma_start(gl_one[:], gl[0:1, :])
         nc.sync.dma_start(v_plane[0][:], v_rows[:, 0, :])
         nc.sync.dma_start(cs_col[:], cs[0:1, :].rearrange("o (p t) -> p (o t)", t=L))
-        nc.sync.dma_start(us_col[:], us.rearrange("(p j) o -> p (j o)", j=L))
-        nc.sync.dma_start(wt_col[:], wt.rearrange("(p j) o -> p (j o)", j=L))
         for t in range(1, L):
             nc.sync.dma_start(v_plane[t][:], v_rows[:, t, :])
         x_rows = x.rearrange("(p j) d -> p j d", j=L)
         x_sb = sb("x_sb", [P, L, N])
         for j in range(L):
             nc.sync.dma_start(x_sb[:, j, :], x_rows[:, j, :])
+        nc.sync.dma_start(us_col[:], us.rearrange("(p j) o -> p (j o)", j=L))
+        nc.sync.dma_start(wt_col[:], wt.rearrange("(p j) o -> p (j o)", j=L))
 
         root_warm = sb("root_warm", [P, 8])
-        nc.gpsimd.memset(root_warm[:, 0:1], 1.0)
+        nc.vector.memset(root_warm[:, 0:1], 1.0)
         nc.scalar.activation(root_warm[:, 4:5], root_warm[:, 0:1], SQRT)
 
         gl_win = sb("gl_win", [P, T])
-        nc.gpsimd.memset(gl_win[:], 0.0)
+        nc.vector.memset(gl_win[:], 0.0)
         nc.scalar.activation(gl_win[0:1, :], gl_one[:], COPY)
 
         y_rows = y.rearrange("(p j) i -> p j i", j=L)
@@ -78,9 +78,8 @@ def tile_attend_gwnorm_v_pl_kernel(tc, vT, x, cs, gl, y, us, wt, offs, out_0, ou
         ident = sb("ident", [P, P])
         make_identity(nc, ident[:])
 
-        win = [sb("win%d" % t, [P, T]) for t in range(L)]
-        for t in range(L):
-            nc.gpsimd.memset(win[t][:], 0.0)
+        win = [sb("win0", [P, T])]
+        nc.vector.memset(win[0][:], 0.0)
 
         cs2_col = sb("cs2_col", [P, L])
         c2_col = sb("c2_col", [P, L])
@@ -188,6 +187,8 @@ def tile_attend_gwnorm_v_pl_kernel(tc, vT, x, cs, gl, y, us, wt, offs, out_0, ou
         first(0)
         for j in range(L):
             x_along_d(j)
+        win.append(sb("win1", [P, T], tag="xtb3"))
+        nc.gpsimd.memset(win[1][:], 0.0)
         first_mm(0)
         lengths(1)
         first(1)
@@ -203,7 +204,7 @@ def tile_attend_gwnorm_v_pl_kernel(tc, vT, x, cs, gl, y, us, wt, offs, out_0, ou
                     nc.vector.tensor_scalar(yc[h][:, j, :], y_sb[h][:, j, :], c2_col[:, j:j + 1], None, MULT)
 
         scale_y(0)
-        xrb = sb("xrb", [P, L, P, L], BF16)
+        xrb = sb("xrb", [P, L, P, L], BF16, tag="nn1")
         for k in range(8):
             qs = slice(16 * k, 16 * (k + 1))
             nc.scalar.copy(xrb[:, :, qs, :].rearrange("p t q j -> p q j t"), x_sb[:].rearrange("p j (q t) -> p q j t", t=L)[:, qs, :, :])
@@ -297,6 +298,9 @@ def tile_attend_gwnorm_v_pl_kernel(tc, vT, x, cs, gl, y, us, wt, offs, out_0, ou
         project(0)
         second(1)
         out_part(0, 0, 2, 2)
+        for name in ("gb1", "gq1"):
+            win.append(sb("win%d" % len(win), [P, T], tag=name))
+            nc.gpsimd.memset(win[-1][:], 0.0)
         project(1)
         scatter(0, 0, 2)
         out_part(0, 2, 4, 3)

@@ -75,10 +75,9 @@ def tile_attend_gwnorm_v_pl_kernel(tc, vT, x, cs, gl, y, us, wt, offs, out_0, ou
         for h in range(2):
             nc.sync.dma_start(y_sb[h][:], y_rows[:, :, h * H:(h + 1) * H])
 
+        win = {0: sb("win0", [P, T])}
         ident = sb("ident", [P, P])
         make_identity(nc, ident[:])
-
-        win = [sb("win0", [P, T])]
         nc.vector.memset(win[0][:], 0.0)
 
         cs2_col = sb("cs2_col", [P, L])
@@ -120,13 +119,14 @@ def tile_attend_gwnorm_v_pl_kernel(tc, vT, x, cs, gl, y, us, wt, offs, out_0, ou
         for t in range(3):
             gather_v(t, 0, L)
             if t == 0:
+                win[3] = sb("win3", [P, T], tag="v_plane0")
+                for k in range(4):
+                    nc.gpsimd.memset(win[3][:, k * C:(k + 1) * C], 0.0)
                 gl_row = sb("gl_row", [P, N])
                 nc.vector.tensor_copy(gl_row[:], gl_win[:].indirect(offsets[:]))
-                gl_ps = bank(6, "gl_ps", [P, L, P])
+                gl_ps = bank(5, "gl_ps", [P, L, P])
                 for m in range(L):
                     nc.tensor.transpose(gl_ps[:, m, :], gl_row[:, blk(m)], ident[:])
-                gl_col = sb("gl_col", [P, L])
-                nc.vector.tensor_copy(gl_col[:], gl_ps[:, :, 0])
             squares(t, 0, L)
             if t == 1:
                 round_pair(0, 0)
@@ -149,7 +149,7 @@ def tile_attend_gwnorm_v_pl_kernel(tc, vT, x, cs, gl, y, us, wt, offs, out_0, ou
                 nc.scalar.activation(nn_junk[:, blk(2 * h + e)], nn_ps[2 * h + e][:], COPY, accum_out=nn[h][:, e:e + 1])
             nc.scalar.activation(length[h][:], nn[h][:], SQRT)
             nc.vector.reciprocal(rlen[h][:], length[h][:])
-            nc.vector.tensor_tensor(s_col[h][:], rlen[h][:], gl_col[:, 2 * h:2 * h + 2], MULT)
+            nc.vector.tensor_tensor(s_col[h][:], rlen[h][:], gl_ps[:, 2 * h:2 * h + 2, 0], MULT)
             s_ps = bank(4 + h, "s_ps%d" % h, [P, 2, P])
             for e in range(2):
                 nc.tensor.transpose(s_ps[:, e, :], s_col[h][:, e:e + 1].to_broadcast([P, P]), ident[:])
@@ -187,7 +187,7 @@ def tile_attend_gwnorm_v_pl_kernel(tc, vT, x, cs, gl, y, us, wt, offs, out_0, ou
         first(0)
         for j in range(L):
             x_along_d(j)
-        win.append(sb("win1", [P, T], tag="xtb3"))
+        win[1] = sb("win1", [P, T], tag="xtb3")
         nc.gpsimd.memset(win[1][:], 0.0)
         first_mm(0)
         lengths(1)
@@ -258,31 +258,58 @@ def tile_attend_gwnorm_v_pl_kernel(tc, vT, x, cs, gl, y, us, wt, offs, out_0, ou
                 nc.vector.scalar_tensor_tensor(junk[m][:], vt_ps[m][:].rearrange("p t q -> p (t q)"), nrnn[h][:, e:e + 1], sbv[m][:], MULT, MULT, accum_out=k_col[m][:])
             for e in range(2):
                 m = 2 * h + e
-                nc.vector.scalar_tensor_tensor(uv[m][:], vt_ps[m][:].rearrange("p t q -> p (t q)"), k_col[m][:], cs2_row[:], MULT, MULT)
+                if h == 0:
+                    nc.vector.scalar_tensor_tensor(uv[m][:], vt_ps[m][:].rearrange("p t q -> p (t q)"), k_col[m][:], cs2_row[:], MULT, MULT)
+                else:
+                    nc.scalar.activation(uv[m][:], vt_ps[m][:].rearrange("p t q -> p (t q)"), COPY, scale=k_col[m][:])
 
-        def turn_back(ps, t, ms):
-            for n, m in enumerate(ms):
-                nc.tensor.matmul(ps[:, n, :], sbv[m][:, blk(t)], ident[:], start=True, stop=False, is_transpose=True)
-                nc.tensor.matmul(ps[:, n, :], uv[m][:, blk(t)], ident[:], start=False, stop=True, is_transpose=True)
+        du = [sb("du%d" % t, [P, N]) for t in range(L)]
+        for t in range(2, L):
+            nc.gpsimd.memset(du[t][:, 0:H], 0.0)
 
-        def out_part(t, lo, hi, n):
-            ps = bank(n, "o_ps%d_%d" % (t, lo), [P, hi - lo, P])
-            turn_back(ps, t, range(lo, hi))
-            nc.scalar.copy(dv[t][:, lo * P:hi * P], ps[:].rearrange("p m i -> p (m i)"))
+        def out0(t, n):
+            ps = bank(n, "o_ps0_%d" % t, [P, 2, P])
+            for m in range(2):
+                nc.tensor.matmul(ps[:, m, :], sbv[m][:, blk(t)], ident[:], start=True, stop=False, is_transpose=True)
+                nc.tensor.matmul(ps[:, m, :], uv[m][:, blk(t)], ident[:], start=False, stop=True, is_transpose=True)
+            nc.scalar.copy(dv[t][:, 0:H], ps[:].rearrange("p m i -> p (m i)"))
 
-        def scatter(t, lo, hi):
-            nc.vector.tensor_copy(win[t][:].indirect(offsets[:, lo * 8:hi * 8]), dv[t][:, lo * P:hi * P])
+        def out1b(ts, n):
+            ps = bank(n, "o_psb_%d" % ts[0], [P, 2, 2, P])
+            for a, t in enumerate(ts):
+                for e in range(2):
+                    nc.tensor.transpose(ps[:, a, e, :], sbv[2 + e][:, blk(t)], ident[:])
+            nc.scalar.copy(dv_all[:].rearrange("p (t n) -> p t n", t=L)[:, ts[0]:ts[0] + 2, H:N], ps[:].rearrange("p a e i -> p a (e i)"))
+
+        def out1u(t, n):
+            ps = bank(n, "o_psu_%d" % t, [P, 2, P])
+            for e in range(2):
+                nc.tensor.transpose(ps[:, e, :], uv[2 + e][:, blk(t)], ident[:])
+            nc.scalar.activation(du[t][:, H:N], ps[:].rearrange("p e i -> p (e i)"), COPY, scale=cs2_col[:, t:t + 1])
+
+        def scatter(t, h):
+            window = win[t][:].indirect(offsets[:, h * 16:(h + 1) * 16])
+            if h == 0:
+                nc.vector.tensor_copy(window, dv[t][:, 0:H])
+            else:
+                nc.vector.tensor_tensor(window, dv[t][:, H:N], du[t][:, H:N], ADD)
+
+        def scatter_all(t):
+            nc.vector.tensor_tensor(win[t][:].indirect(offsets[:]), dv[t], du[t][:], ADD)
 
         o_rows = out_0.rearrange("(p t) c -> p t c", t=L)
-        edges = [0, 256, 512, 1024, 1536, 2048]
-        chunks = [(edges[c], edges[c + 1]) for c in range(5)]
-        pairs = [sb("pairs%d" % c, [P, 2, hi - lo, 2], BF16, tag=["v_plane0", "v_plane1", "v_plane2", "v_plane3", "gl_win"][c]) for c, (lo, hi) in enumerate(chunks)]
+        edges = [0,512,1024,1536,1792,2048]
+        chunks = [(edges[c], edges[c + 1]) for c in range(len(edges) - 1)]
+        pairs = [sb("pairs%d" % c, [P, 2, hi - lo, 2], BF16, tag=["y_sb0", "v_plane1", "v_plane2", "v_plane3", "gl_win", "x_sb"][c]) for c, (lo, hi) in enumerate(chunks)]
 
         def round_plane(t):
             for c, (lo, hi) in enumerate(chunks):
-                if t >= 2 and c < NV:
-                    nc.vector.tensor_copy(pairs[c][:, t // 2, :, t % 2], win[t][:, lo:hi])
-                else:
+                if t == 3 and c < NV:
+                    nc.vector.tensor_copy(pairs[c][:, 1, :, 0], win[2][:, lo:hi])
+            for c, (lo, hi) in enumerate(chunks):
+                if t == 3 and c < NV:
+                    nc.vector.tensor_copy(pairs[c][:, 1, :, 1], win[3][:, lo:hi])
+                elif t < 2 or c >= NV:
                     nc.scalar.copy(pairs[c][:, t // 2, :, t % 2], win[t][:, lo:hi])
 
         scale_a(0)
@@ -297,32 +324,38 @@ def tile_attend_gwnorm_v_pl_kernel(tc, vT, x, cs, gl, y, us, wt, offs, out_0, ou
         turn_v(1)
         project(0)
         second(1)
-        out_part(0, 0, 2, 2)
-        for name in ("gb1", "gq1"):
-            win.append(sb("win%d" % len(win), [P, T], tag=name))
-            nc.gpsimd.memset(win[-1][:], 0.0)
+        out0(0, 2)
+        out0(1, 3)
+        win[2] = sb("win2", [P, T], tag="gb1")
+        nc.gpsimd.memset(win[2][:], 0.0)
         project(1)
-        scatter(0, 0, 2)
-        out_part(0, 2, 4, 3)
-        out_part(1, 0, 4, 4)
-        out_part(2, 0, 4, 5)
-        out_part(3, 0, 4, 6)
-        scatter(0, 2, 4)
+        out1b((0, 1), 4)
+        out1u(0, 6)
+        out1u(1, 7)
+        out1b((2, 3), 5)
+        out0(2, 2)
+        out0(3, 3)
+        out1u(2, 0)
+        out1u(3, 1)
+        scatter(0, 0)
+        scatter(1, 0)
+        scatter(0, 1)
         nc.sync.dma_start(o_rows[:, 0, :], win[0][:])
         round_plane(0)
-        scatter(1, 0, 4)
+        scatter(1, 1)
         nc.sync.dma_start(o_rows[:, 1, :], win[1][:])
         round_plane(1)
-        scatter(2, 0, 4)
+        scatter_all(2)
         nc.sync.dma_start(o_rows[:, 2, :], win[2][:])
         round_plane(2)
-        scatter(3, 0, 4)
+        scatter_all(3)
         nc.sync.dma_start(o_rows[:, 3, :], win[3][:])
 
         o_words = out_1[0].rearrange("p c l -> p (c l)").bitcast(I32)
         o_scales = sb("o_scales", [P, T], U8)
         ob = [sb("ob%d" % c, [P, (hi - lo) * L], BF16) for c, (lo, hi) in enumerate(chunks)]
-        oq = [sb("oq%d" % k, [P, C], U32) for k in range(4)]
+        oq_first = sb("oq_first", [P, 2 * C], U32)
+        oq = [oq_first[:, lo:hi] if c < 2 else sb("oq%d" % c, [P, hi - lo], U32)[:] for c, (lo, hi) in enumerate(chunks)]
 
         def weave(c, eng):
             dst = ob[c][:].bitcast(F32).rearrange("p (c i u) -> p c u i", i=4, u=2)
@@ -334,21 +367,22 @@ def tile_attend_gwnorm_v_pl_kernel(tc, vT, x, cs, gl, y, us, wt, offs, out_0, ou
 
         def finish(c):
             lo, hi = chunks[c]
-            k = lo // C
-            nc.vector.quantize_mx(oq[k][:, lo - k * C:hi - k * C].bitcast(E4M3), o_scales[:, lo:hi], ob[c][:])
-            if hi % C == 0:
-                nc.sync.dma_start(o_words[:, k * C:(k + 1) * C], oq[k][:].bitcast(I32))
+            nc.vector.quantize_mx(oq[c].bitcast(E4M3), o_scales[:, lo:hi], ob[c][:])
+            if c == 1:
+                nc.sync.dma_start(o_words[:, 0:hi], oq_first[:].bitcast(I32))
+            elif c > 1:
+                nc.sync.dma_start(o_words[:, lo:hi], oq[c].bitcast(I32))
 
         round_plane(3)
+        weave(2, "s")
+        weave(4, "s")
         weave(0, "v")
         weave(1, "v")
         finish(0)
-        weave(2, "v")
-        finish(1)
-        weave(4, "s")
         weave(3, "v")
-        finish(2)
+        finish(1)
         finish(3)
+        finish(2)
         finish(4)
         for q in range(4):
             (nc.scalar if q % 2 else nc.sync).dma_start(out_2[0, 4 * q:4 * q + 4, :].bitcast(I32), o_scales[32 * q:32 * q + 4, :].bitcast(I32))

import concourse.mybir as mybir
from concourse.masks import make_identity

FLOPS = 536870912

F32 = mybir.dt.float32
BF16 = mybir.dt.bfloat16
I32 = mybir.dt.int32
U32 = mybir.dt.uint32
U16 = mybir.dt.uint16
U8 = mybir.dt.uint8
E4M3 = mybir.dt.float8_e4m3fn_x4
E5M2 = mybir.dt.float8_e5m2_x4
MULT = mybir.AluOpType.mult
ADD = mybir.AluOpType.add
SUBTRACT = mybir.AluOpType.subtract
COPY = mybir.ActivationFunctionType.Copy
SQUARE = mybir.ActivationFunctionType.Square
SQRT = mybir.ActivationFunctionType.Sqrt

P = 128
L = 4
N = 512
T = 2048
H = 256
C = 512
NV = 2
YC = "vs"


def tile_attend_gwnorm_v_pl_kernel(tc, vT, x, cs, gl, y, us, wt, offs, out_0, out_1, out_2):
    nc = tc.nc
    with tc.tile_pool(name="keep", bufs=1) as keep, tc.psum_pool(name="psum", bufs=1) as psum:

        def sb(name, shape, dtype=F32, tag=None):
            return keep.tile(shape, dtype, name=name, tag=tag or name, align_bytes=64)

        def bank(n, name, shape):
            return psum.tile(shape, F32, name=name, tag="bank%d" % n)

        def blk(m):
            return slice(m * P, (m + 1) * P)

        offsets = keep.tile([P, N // 16], U16, name="offsets")
        nc.sync.dma_start(offsets[:], offs)

        v_rows = vT.rearrange("(p t) c -> p t c", t=L)
        v_plane = [sb("v_plane%d" % t, [P, T]) for t in range(L)]
        cs_col = sb("cs_col", [P, L])
        us_col = sb("us_col", [P, L])
        wt_col = sb("wt_col", [P, L])
        gl_one = sb("gl_one", [1, T], tag="dv")
        nc.sync.dma_start(gl_one[:], gl[0:1, :])
        nc.sync.dma_start(v_plane[0][:], v_rows[:, 0, :])
        nc.sync.dma_start(cs_col[:], cs[0:1, :].rearrange("o (p t) -> p (o t)", t=L))
        for t in range(1, L):
            nc.sync.dma_start(v_plane[t][:], v_rows[:, t, :])
        x_rows = x.rearrange("(p j) d -> p j d", j=L)
        x_sb = sb("x_sb", [P, L, N])
        for j in range(L):
            nc.sync.dma_start(x_sb[:, j, :], x_rows[:, j, :])
        nc.sync.dma_start(us_col[:], us.rearrange("(p j) o -> p (j o)", j=L))
        nc.sync.dma_start(wt_col[:], wt.rearrange("(p j) o -> p (j o)", j=L))

        root_warm = sb("root_warm", [P, 8])
        nc.vector.memset(root_warm[:, 0:1], 1.0)
        nc.scalar.activation(root_warm[:, 4:5], root_warm[:, 0:1], SQRT)

        gl_win = sb("gl_win", [P, T])
        nc.vector.memset(gl_win[:], 0.0)
        nc.scalar.activation(gl_win[0:1, :], gl_one[:], COPY)

        y_rows = y.rearrange("(p j) i -> p j i", j=L)
        y_sb = [sb("y_sb%d" % h, [P, L, H]) for h in range(2)]
        for h in range(2):
            nc.sync.dma_start(y_sb[h][:], y_rows[:, :, h * H:(h + 1) * H])

        win = {0: sb("win0", [P, T])}
        ident = sb("ident", [P, P])
        make_identity(nc, ident[:])
        nc.vector.memset(win[0][:], 0.0)

        cs2_col = sb("cs2_col", [P, L])
        c2_col = sb("c2_col", [P, L])
        c1_col = sb("c1_col", [P, L])
        nc.vector.tensor_tensor(cs2_col[:], cs_col[:], cs_col[:], MULT)
        nc.vector.tensor_tensor(c2_col[:], wt_col[:], us_col[:], MULT)
        nc.vector.tensor_tensor(c1_col[:], c2_col[:], us_col[:], MULT)

        g_all = [sb("g_all%d" % u, [P, 2 * N]) for u in range(2)]
        vb = [sb("vb%d" % h, [P, H, L], BF16) for h in range(2)]
        cs2_ps = bank(4, "cs2_ps", [P, L, P])
        for t in range(L):
            nc.tensor.transpose(cs2_ps[:, t, :], cs2_col[:, t:t + 1].to_broadcast([P, P]), ident[:])
        cs2_row = sb("cs2_row", [P, N])
        nc.scalar.copy(cs2_row[:], cs2_ps[:].rearrange("p t q -> p (t q)"))
        nn_ps = [bank(m, "nn_ps%d" % m, [P, P]) for m in range(L)]
        sq = [sb("sq%d" % t, [P, N]) for t in range(L)]

        def gathered(t, lo, hi):
            return g_all[t // 2][:, (t % 2) * N + lo * P:(t % 2) * N + hi * P]

        def gather_v(t, lo, hi):
            nc.vector.tensor_copy(gathered(t, lo, hi), v_plane[t][:].indirect(offsets[:, lo * 8:hi * 8]))

        def squares(t, lo, hi):
            nc.scalar.activation(sq[t][:, lo * P:hi * P], gathered(t, lo, hi), SQUARE, scale=cs_col[:, t:t + 1])
            for m in range(lo, hi):
                nc.tensor.matmul(nn_ps[m][:], sq[t][:, blk(m)], ident[:], start=(t == 0), stop=(t == L - 1), is_transpose=True)

        def round_pair(u, h):
            dst = vb[h][:, :, 2 * u:2 * u + 2].rearrange("p (c i) e -> p c e i", i=4)
            src = g_all[u][:].rearrange("p (e n) -> p e n", e=2)[:, :, h * H:(h + 1) * H].rearrange("p e (c i) -> p c e i", i=4)
            if u == 0:
                nc.scalar.copy(dst, src)
            else:
                nc.vector.tensor_copy(dst, src)

        for t in range(3):
            gather_v(t, 0, L)
            if t == 0:
                win[3] = sb("win3", [P, T], tag="v_plane0")
                for k in range(4):
                    nc.gpsimd.memset(win[3][:, k * C:(k + 1) * C], 0.0)
                gl_row = sb("gl_row", [P, N])
                nc.vector.tensor_copy(gl_row[:], gl_win[:].indirect(offsets[:]))
                gl_ps = bank(5, "gl_ps", [P, L, P])
                for m in range(L):
                    nc.tensor.transpose(gl_ps[:, m, :], gl_row[:, blk(m)], ident[:])
            squares(t, 0, L)
            if t == 1:
                round_pair(0, 0)
                round_pair(0, 1)

        vq = [sb("vq%d" % h, [P, H], U32) for h in range(2)]
        vs = [sb("vs%d" % h, [P, H], U8) for h in range(2)]
        nn = [sb("nn%d" % h, [P, 2]) for h in range(2)]
        nn_junk = sb("nn_junk", [P, N])
        length = [sb("length%d" % h, [P, 2]) for h in range(2)]
        rlen = [sb("rlen%d" % h, [P, 2]) for h in range(2)]
        s_col = [sb("s_col%d" % h, [P, 2]) for h in range(2)]
        nrnn = [sb("nrnn%d" % h, [P, 2]) for h in range(2)]
        s_row = [sb("s_row%d" % h, [P, H]) for h in range(2)]
        yc = [sb("yc%d" % h, [P, L, H]) for h in range(2)]
        a_ps = [None] * L

        def lengths(h):
            for e in range(2):
                nc.scalar.activation(nn_junk[:, blk(2 * h + e)], nn_ps[2 * h + e][:], COPY, accum_out=nn[h][:, e:e + 1])
            nc.scalar.activation(length[h][:], nn[h][:], SQRT)
            nc.vector.reciprocal(rlen[h][:], length[h][:])
            nc.vector.tensor_tensor(s_col[h][:], rlen[h][:], gl_ps[:, 2 * h:2 * h + 2, 0], MULT)
            s_ps = bank(4 + h, "s_ps%d" % h, [P, 2, P])
            for e in range(2):
                nc.tensor.transpose(s_ps[:, e, :], s_col[h][:, e:e + 1].to_broadcast([P, P]), ident[:])
            nc.scalar.copy(s_row[h][:], s_ps[:].rearrange("p m i -> p (m i)"))

        def first(h):
            round_pair(1, h)
            nc.vector.quantize_mx(vq[h][:].bitcast(E4M3), vs[h][:], vb[h][:].rearrange("p i t -> p (i t)"))

        def first_mm(h):
            for u in range(2):
                a_ps[2 * h + u] = bank(2 * h + u, "a_ps%d_%d" % (h, u), [P, 2, H])
                for e in range(2):
                    j = 2 * u + e
                    nc.tensor.matmul_mx(a_ps[2 * h + u][:, e, :], lhsT=xq[j][:].bitcast(E4M3), lhsT_scale=xs[j][:], rhs=vq[h][:].bitcast(E4M3), rhs_scale=vs[h][:], start=True, stop=True)

        xq = [sb("xq%d" % j, [P, P], U32) for j in range(L)]
        xs = [sb("xs%d" % j, [P, P], U8) for j in range(L)]

        def x_along_d(j):
            xb = sb("xb%d" % j, [P, 2, P, 2], BF16)
            nc.vector.tensor_copy(xb[:].rearrange("p u q e -> p q u e"), x_sb[:, j, :].rearrange("p (q u e) -> p q u e", u=2, e=2))
            words = xb[:].rearrange("p u q e -> p (u q e)").bitcast(F32)
            ps = bank(6 + j % 2, "xt_ps%d" % j, [P, 2, P])
            for u in range(2):
                nc.tensor.transpose(ps[:, u, :], words[:, blk(u)], ident[:])
            xtb = sb("xtb%d" % j, [P, N], BF16)
            nc.scalar.copy(xtb[:].bitcast(F32).rearrange("q (p u) -> q p u", u=2), ps[:].rearrange("q u p -> q p u"))
            nc.vector.quantize_mx(xq[j][:].bitcast(E4M3), xs[j][:], xtb[:])

        for h in range(2):
            gather_v(3, 2 * h, 2 * h + 2)
            squares(3, 2 * h, 2 * h + 2)
        lengths(0)
        first(0)
        for j in range(L):
            x_along_d(j)
        win[1] = sb("win1", [P, T], tag="xtb3")
        nc.gpsimd.memset(win[1][:], 0.0)
        first_mm(0)
        lengths(1)
        first(1)
        first_mm(1)

        def scale_y(h):
            for j in range(L):
                if YC[h] == "g":
                    nc.gpsimd.tensor_scalar(yc[h][:, j, :], y_sb[h][:, j, :], c2_col[:, j:j + 1], 0.0, MULT, ADD)
                elif YC[h] == "s":
                    nc.scalar.activation(yc[h][:, j, :], y_sb[h][:, j, :], COPY, scale=c2_col[:, j:j + 1])
                else:
                    nc.vector.tensor_scalar(yc[h][:, j, :], y_sb[h][:, j, :], c2_col[:, j:j + 1], None, MULT)

        scale_y(0)
        xrb = sb("xrb", [P, L, P, L], BF16, tag="nn1")
        for k in range(8):
            qs = slice(16 * k, 16 * (k + 1))
            nc.scalar.copy(xrb[:, :, qs, :].rearrange("p t q j -> p q j t"), x_sb[:].rearrange("p j (q t) -> p q j t", t=L)[:, qs, :, :])
        xrq = sb("xrq", [P, N], U32)
        xrs = sb("xrs", [P, N], U8)

        scale_y(1)
        for h in range(2):
            nc.vector.scalar_tensor_tensor(nrnn[h][:], rlen[h][:], -1.0, rlen[h][:], MULT, MULT)

        vt_ps = [None] * L

        def turn_v(h):
            for e in range(2):
                m = 2 * h + e
                vt_ps[m] = bank([4, 5, 0, 1][m], "vt_ps%d" % m, [P, L, P])
                for t in range(L):
                    nc.tensor.transpose(vt_ps[m][:, t, :], gathered(t, m, m + 1), ident[:])

        gq = [sb("gq%d" % h, [P, H], U32) for h in range(2)]
        gs = [sb("gs%d" % h, [P, H], U8) for h in range(2)]
        gb = [sb("gb%d" % h, [P, H, L], BF16) for h in range(2)]
        t1 = [sb("t1_%d" % h, [P, L, H]) for h in range(2)]
        sbv = [sb("sb%d" % m, [P, N]) for m in range(L)]
        uv = [sb("u%d" % m, [P, N]) for m in range(L)]
        junk = [sb("junk%d" % m, [P, N], tag="sq%d" % m) for m in range(L)]
        k_col = [sb("k%d" % m, [P, 1]) for m in range(L)]
        dv_all = sb("dv", [P, L * N])
        dv = [dv_all[:, t * N:(t + 1) * N] for t in range(L)]

        def scale_a(h):
            for j in range(L):
                nc.vector.scalar_tensor_tensor(t1[h][:, j, :], a_ps[2 * h + j // 2][:, j % 2, :], c1_col[:, j:j + 1], s_row[h][:], MULT, MULT)

        def make_g(h):
            nc.vector.tensor_tensor(gb[h][:].rearrange("p (c i) j -> p c j i", i=4), t1[h][:].rearrange("p j (c i) -> p c j i", i=4), yc[h][:].rearrange("p j (c i) -> p c j i", i=4), SUBTRACT)

        def second_q(h):
            nc.vector.quantize_mx(gq[h][:].bitcast(E5M2), gs[h][:], gb[h][:].rearrange("p i j -> p (i j)"))

        def second(h):
            for e in range(2):
                m = 2 * h + e
                b_ps = bank(6 + e, "b_ps%d" % m, [P, N])
                nc.tensor.matmul_mx(b_ps[:], lhsT=gq[h][:, blk(e)].bitcast(E5M2), lhsT_scale=gs[h][:, blk(e)], rhs=xrq[:].bitcast(E4M3), rhs_scale=xrs[:], start=True, stop=True)
                nc.scalar.activation(sbv[m][:], b_ps[:], COPY, scale=s_col[h][:, e:e + 1])

        def project(h):
            for e in range(2):
                m = 2 * h + e
                nc.vector.scalar_tensor_tensor(junk[m][:], vt_ps[m][:].rearrange("p t q -> p (t q)"), nrnn[h][:, e:e + 1], sbv[m][:], MULT, MULT, accum_out=k_col[m][:])
            for e in range(2):
                m = 2 * h + e
                if h == 0:
                    nc.vector.scalar_tensor_tensor(uv[m][:], vt_ps[m][:].rearrange("p t q -> p (t q)"), k_col[m][:], cs2_row[:], MULT, MULT)
                else:
                    nc.scalar.activation(uv[m][:], vt_ps[m][:].rearrange("p t q -> p (t q)"), COPY, scale=k_col[m][:])

        du = [sb("du%d" % t, [P, N]) for t in range(L)]
        for t in range(2, L):
            nc.gpsimd.memset(du[t][:, 0:H], 0.0)

        def out0(t, n):
            ps = bank(n, "o_ps0_%d" % t, [P, 2, P])
            for m in range(2):
                nc.tensor.matmul(ps[:, m, :], sbv[m][:, blk(t)], ident[:], start=True, stop=False, is_transpose=True)
                nc.tensor.matmul(ps[:, m, :], uv[m][:, blk(t)], ident[:], start=False, stop=True, is_transpose=True)
            nc.scalar.copy(dv[t][:, 0:H], ps[:].rearrange("p m i -> p (m i)"))

        def out1b(ts, n):
            ps = bank(n, "o_psb_%d" % ts[0], [P, 2, 2, P])
            for a, t in enumerate(ts):
                for e in range(2):
                    nc.tensor.transpose(ps[:, a, e, :], sbv[2 + e][:, blk(t)], ident[:])
            nc.scalar.copy(dv_all[:].rearrange("p (t n) -> p t n", t=L)[:, ts[0]:ts[0] + 2, H:N], ps[:].rearrange("p a e i -> p a (e i)"))

        def out1u(t, n):
            ps = bank(n, "o_psu_%d" % t, [P, 2, P])
            for e in range(2):
                nc.tensor.transpose(ps[:, e, :], uv[2 + e][:, blk(t)], ident[:])
            nc.scalar.activation(du[t][:, H:N], ps[:].rearrange("p e i -> p (e i)"), COPY, scale=cs2_col[:, t:t + 1])

        def scatter(t, h):
            window = win[t][:].indirect(offsets[:, h * 16:(h + 1) * 16])
            if h == 0:
                nc.vector.tensor_copy(window, dv[t][:, 0:H])
            else:
                nc.vector.tensor_tensor(window, dv[t][:, H:N], du[t][:, H:N], ADD)

        def scatter_all(t):
            nc.vector.tensor_tensor(win[t][:].indirect(offsets[:]), dv[t], du[t][:], ADD)

        o_rows = out_0.rearrange("(p t) c -> p t c", t=L)
        edges = [0,512,1024,1536,1792,2048]
        chunks = [(edges[c], edges[c + 1]) for c in range(len(edges) - 1)]
        pairs = [sb("pairs%d" % c, [P, 2, hi - lo, 2], BF16, tag=["y_sb0", "v_plane1", "v_plane2", "v_plane3", "gl_win", "x_sb"][c]) for c, (lo, hi) in enumerate(chunks)]

        def round_plane(t):
            for c, (lo, hi) in enumerate(chunks):
                if t == 3 and c < NV:
                    nc.vector.tensor_copy(pairs[c][:, 1, :, 0], win[2][:, lo:hi])
            for c, (lo, hi) in enumerate(chunks):
                if t == 3 and c < NV:
                    nc.vector.tensor_copy(pairs[c][:, 1, :, 1], win[3][:, lo:hi])
                elif t < 2 or c >= NV:
                    nc.scalar.copy(pairs[c][:, t // 2, :, t % 2], win[t][:, lo:hi])

        scale_a(0)
        make_g(0)
        nc.vector.quantize_mx(xrq[:].bitcast(E4M3), xrs[:], xrb[:].rearrange("p t q j -> p (t q j)"))
        second_q(0)
        second(0)
        turn_v(0)
        scale_a(1)
        make_g(1)
        second_q(1)
        turn_v(1)
        project(0)
        second(1)
        out0(0, 2)
        out0(1, 3)
        win[2] = sb("win2", [P, T], tag="gb1")
        nc.gpsimd.memset(win[2][:], 0.0)
        project(1)
        out1b((0, 1), 4)
        out1u(0, 6)
        out1u(1, 7)
        out1b((2, 3), 5)
        out0(2, 2)
        out0(3, 3)
        out1u(2, 0)
        out1u(3, 1)
        scatter(0, 0)
        scatter(1, 0)
        scatter(0, 1)
        nc.sync.dma_start(o_rows[:, 0, :], win[0][:])
        round_plane(0)
        scatter(1, 1)
        nc.sync.dma_start(o_rows[:, 1, :], win[1][:])
        round_plane(1)
        scatter_all(2)
        nc.sync.dma_start(o_rows[:, 2, :], win[2][:])
        round_plane(2)
        scatter_all(3)
        nc.sync.dma_start(o_rows[:, 3, :], win[3][:])

        o_words = out_1[0].rearrange("p c l -> p (c l)").bitcast(I32)
        o_scales = sb("o_scales", [P, T], U8)
        ob = [sb("ob%d" % c, [P, (hi - lo) * L], BF16) for c, (lo, hi) in enumerate(chunks)]
        oq_first = sb("oq_first", [P, 2 * C], U32)
        oq = [oq_first[:, lo:hi] if c < 2 else sb("oq%d" % c, [P, hi - lo], U32)[:] for c, (lo, hi) in enumerate(chunks)]

        def weave(c, eng):
            dst = ob[c][:].bitcast(F32).rearrange("p (c i u) -> p c u i", i=4, u=2)
            src = pairs[c][:].rearrange("p u c e -> p (u c e)").bitcast(F32).rearrange("p (u c i) -> p c u i", u=2, i=4)
            if eng == "v":
                nc.vector.tensor_copy(dst, src)
            else:
                nc.scalar.copy(dst, src)

        def finish(c):
            lo, hi = chunks[c]
            nc.vector.quantize_mx(oq[c].bitcast(E4M3), o_scales[:, lo:hi], ob[c][:])
            if c == 1:
                nc.sync.dma_start(o_words[:, 0:hi], oq_first[:].bitcast(I32))
            elif c > 1:
                nc.sync.dma_start(o_words[:, lo:hi], oq[c].bitcast(I32))

        round_plane(3)
        weave(2, "s")
        weave(4, "s")
        weave(0, "v")
        weave(1, "v")
        finish(0)
        weave(3, "v")
        finish(1)
        finish(3)
        finish(2)
        finish(4)
        for q in range(4):
            (nc.scalar if q % 2 else nc.sync).dma_start(out_2[0, 4 * q:4 * q + 4, :].bitcast(I32), o_scales[32 * q:32 * q + 4, :].bitcast(I32))
